import numpy as np
import ml_dtypes

BF16 = ml_dtypes.bfloat16


def bf(x):
    return np.asarray(x, np.float32).astype(BF16)


def f32(x):
    return np.asarray(x, np.float32)


def f64(x):
    return np.asarray(x).astype(np.float64)


def striped(idx):
    return np.tile(idx.reshape(-1, 16).T, (8, 1))


A, S, K, M, N, E, Q = 256, 256, 128, 512, 256, 4, 64


def setup_inputs():
    return {"a": bf(np.random.standard_normal((A, S))), "wd": bf(np.random.standard_normal((A, M)) / np.sqrt(A)), "x": bf(np.random.standard_normal((K, N))), "w": bf(1.2 * np.random.standard_normal((E, K, M)) / np.sqrt(K)), "s": f32(0.5 + np.random.random_sample((M, 1))), "offs": striped(np.random.permutation(S))}


def reference(a, wd, x, w, s, offs):
    idx = offs[:16].T.reshape(-1)
    z = f64(wd).T @ f64(a)
    for e in range(E):
        z[:, idx[e * Q : (e + 1) * Q]] += f64(w)[e].T @ f64(x)[:, e * Q : (e + 1) * Q]
    z = z / np.sqrt((z**2).mean(axis=0, keepdims=True) + 1e-5) * f64(s)
    return z

@@ -1,0 +1,78 @@
+import concourse.mybir as mybir
+
+BF16, F32, U16 = mybir.dt.bfloat16, mybir.dt.float32, mybir.dt.uint16
+ADD, MULT = mybir.AluOpType.add, mybir.AluOpType.mult
+SQUARE = mybir.ActivationFunctionType.Square
+ABS_RSQRT = mybir.ActivationFunctionType.Abs_reciprocal_sqrt
+
+P = 128
+D = 256
+M = 512
+N = 256
+K = 128
+E = 4
+Q = N // E
+EPS = 1e-5
+DB = D // P
+MB = M // P
+
+FLOPS = 2 * D * M * N + 2 * K * M * N + 4 * M * N
+
+
+def tile_rows_placenorm_proj_kernel(tc, a, wd, x, w, s, offs, out):
+    nc = tc.nc
+    with (
+        tc.tile_pool(name="held", bufs=1) as held,
+        tc.psum_pool(name="psum", bufs=1) as psum,
+    ):
+        a_tile = held.tile([P, DB, N], BF16)
+        wd_tile = held.tile([P, DB, M], BF16)
+        offsets = held.tile([P, N // 16], U16)
+        x_tile = held.tile([P, N], BF16)
+        w_tile = held.tile([P, E, M], BF16)
+        gain = held.tile([P, MB], F32)
+        nc.sync.dma_start(a_tile[:], a.rearrange("(p t) n -> p t n", t=DB))
+        nc.sync.dma_start(wd_tile[:], wd.rearrange("(p t) m -> p t m", t=DB))
+        nc.sync.dma_start(offsets[:], offs)
+        nc.sync.dma_start(x_tile[:], x)
+        nc.sync.dma_start(w_tile[:], w.rearrange("e k m -> k e m"))
+        nc.sync.dma_start(gain[:], s.rearrange("(b p) o -> p (b o)", p=P))
+
+        mean_weights = held.tile([P, P], BF16)
+        nc.vector.memset(mean_weights[:], 1.0 / M)
+        eps = held.tile([P, 1], F32)
+        nc.vector.memset(eps[:], EPS)
+
+        windows = [psum.tile([P, N], F32, name=f"window{b}") for b in range(MB)]
+        for b in range(MB):
+            for t in range(DB):
+                nc.tensor.matmul(
+                    windows[b][:], wd_tile[:, t, b * P : (b + 1) * P], a_tile[:, t, :],
+                    start=(t == 0), stop=False,
+                )
+
+        for b in range(MB):
+            for e in range(E):
+                piece = offsets[:, e * (Q // 16) : (e + 1) * (Q // 16)]
+                nc.tensor.matmul(
+                    windows[b][:].indirect(piece),
+                    w_tile[:, e, b * P : (b + 1) * P],
+                    x_tile[:, e * Q : (e + 1) * Q],
+                    start=False, stop=(e == E - 1),
+                )
+
+        squares = held.tile([P, MB, N], BF16)
+        for b in range(MB):
+            nc.scalar.activation(squares[:, b, :], windows[b][:], SQUARE)
+        mean = psum.tile([P, N], F32)
+        for b in range(MB):
+            nc.tensor.matmul(mean[:], mean_weights[:], squares[:, b, :], start=(b == 0), stop=(b == MB - 1))
+
+        inverse_rms = held.tile([P, N], F32)
+        nc.scalar.activation(inverse_rms[:], mean[:], ABS_RSQRT, bias=eps[:])
+        normed = held.tile([P, MB, N], F32)
+        for b in range(MB):
+            nc.vector.scalar_tensor_tensor(
+                normed[:, b, :], windows[b][:], gain[:, b : b + 1], inverse_rms[:], MULT, MULT
+            )
+            nc.sync.dma_start(out[b * P : (b + 1) * P, :], normed[:, b, :])

@@ -1,7 +1,7 @@
 import concourse.mybir as mybir
 
 BF16, F32, U16 = mybir.dt.bfloat16, mybir.dt.float32, mybir.dt.uint16
-ADD, MULT = mybir.AluOpType.add, mybir.AluOpType.mult
+MULT = mybir.AluOpType.mult
 SQUARE = mybir.ActivationFunctionType.Square
 ABS_RSQRT = mybir.ActivationFunctionType.Abs_reciprocal_sqrt
 
@@ -13,6 +13,8 @@ K = 128
 E = 4
 Q = N // E
 EPS = 1e-5
+WARM_COLUMNS = 512
+WARM_MATMULS = 5
 DB = D // P
 MB = M // P
 
@@ -36,18 +38,24 @@ def tile_rows_placenorm_proj_kernel(tc, a, wd, x, w, s, offs, out):
         nc.sync.dma_start(offsets[:], offs)
         nc.sync.dma_start(x_tile[:], x)
         nc.sync.dma_start(w_tile[:], w.rearrange("e k m -> k e m"))
-        nc.sync.dma_start(gain[:], s.rearrange("(b p) o -> p (b o)", p=P))
+        nc.sync.dma_start(gain[:], s.rearrange("(p b) o -> p (b o)", b=MB))
 
         mean_weights = held.tile([P, P], BF16)
         nc.vector.memset(mean_weights[:], 1.0 / M)
         eps = held.tile([P, 1], F32)
         nc.vector.memset(eps[:], EPS)
 
+        zeros = held.tile([P, WARM_COLUMNS], BF16)
+        nc.gpsimd.memset(zeros[:], 0.0)
+        warm_bank = psum.tile([P, WARM_COLUMNS], F32)
+        for i in range(WARM_MATMULS):
+            nc.tensor.matmul(warm_bank[:], zeros[:, 0:P], zeros[:], start=True, stop=True)
+
         windows = [psum.tile([P, N], F32, name=f"window{b}") for b in range(MB)]
-        for b in range(MB):
-            for t in range(DB):
+        for t in range(DB):
+            for b in range(MB):
                 nc.tensor.matmul(
-                    windows[b][:], wd_tile[:, t, b * P : (b + 1) * P], a_tile[:, t, :],
+                    windows[b][:], wd_tile[:, t, b::MB], a_tile[:, t, :],
                     start=(t == 0), stop=False,
                 )
 
@@ -56,7 +64,7 @@ def tile_rows_placenorm_proj_kernel(tc, a, wd, x, w, s, offs, out):
                 piece = offsets[:, e * (Q // 16) : (e + 1) * (Q // 16)]
                 nc.tensor.matmul(
                     windows[b][:].indirect(piece),
-                    w_tile[:, e, b * P : (b + 1) * P],
+                    w_tile[:, e, b::MB],
                     x_tile[:, e * Q : (e + 1) * Q],
                     start=False, stop=(e == E - 1),
                 )
@@ -71,8 +79,10 @@ def tile_rows_placenorm_proj_kernel(tc, a, wd, x, w, s, offs, out):
         inverse_rms = held.tile([P, N], F32)
         nc.scalar.activation(inverse_rms[:], mean[:], ABS_RSQRT, bias=eps[:])
         normed = held.tile([P, MB, N], F32)
+        out_rows = out.rearrange("(p b) n -> p b n", b=MB)
         for b in range(MB):
             nc.vector.scalar_tensor_tensor(
                 normed[:, b, :], windows[b][:], gain[:, b : b + 1], inverse_rms[:], MULT, MULT
             )
-            nc.sync.dma_start(out[b * P : (b + 1) * P, :], normed[:, b, :])
+            if b % 2 == 1:
+                nc.sync.dma_start(out_rows[:, b - 1 : b + 1, :], normed[:, b - 1 : b + 1, :])

@@ -14,7 +14,7 @@ E = 4
 Q = N // E
 EPS = 1e-5
 WARM_COLUMNS = 512
-WARM_MATMULS = 5
+WARM_MATMULS = 4
 DB = D // P
 MB = M // P
 
@@ -38,15 +38,19 @@ def tile_rows_placenorm_proj_kernel(tc, a, wd, x, w, s, offs, out):
         nc.sync.dma_start(offsets[:], offs)
         nc.sync.dma_start(x_tile[:], x)
         nc.sync.dma_start(w_tile[:], w.rearrange("e k m -> k e m"))
-        nc.sync.dma_start(gain[:], s.rearrange("(p b) o -> p (b o)", b=MB))
+        nc.sync.dma_start(gain[:], s.rearrange("(b p) o -> p (b o)", p=P))
+
+        zeros = held.tile([P, WARM_COLUMNS], BF16)
+        nc.vector.memset(zeros[:], 0.0)
 
         mean_weights = held.tile([P, P], BF16)
         nc.vector.memset(mean_weights[:], 1.0 / M)
         eps = held.tile([P, 1], F32)
         nc.vector.memset(eps[:], EPS)
 
-        zeros = held.tile([P, WARM_COLUMNS], BF16)
-        nc.gpsimd.memset(zeros[:], 0.0)
+        table_load = held.tile([P, 1], F32)
+        nc.scalar.activation(table_load[:], eps[:], ABS_RSQRT, bias=eps[:])
+
         warm_bank = psum.tile([P, WARM_COLUMNS], F32)
         for i in range(WARM_MATMULS):
             nc.tensor.matmul(warm_bank[:], zeros[:, 0:P], zeros[:], start=True, stop=True)
@@ -55,7 +59,7 @@ def tile_rows_placenorm_proj_kernel(tc, a, wd, x, w, s, offs, out):
         for t in range(DB):
             for b in range(MB):
                 nc.tensor.matmul(
-                    windows[b][:], wd_tile[:, t, b::MB], a_tile[:, t, :],
+                    windows[b][:], wd_tile[:, t, b * P : (b + 1) * P], a_tile[:, t, :],
                     start=(t == 0), stop=False,
                 )
 
@@ -64,7 +68,7 @@ def tile_rows_placenorm_proj_kernel(tc, a, wd, x, w, s, offs, out):
                 piece = offsets[:, e * (Q // 16) : (e + 1) * (Q // 16)]
                 nc.tensor.matmul(
                     windows[b][:].indirect(piece),
-                    w_tile[:, e, b::MB],
+                    w_tile[:, e, b * P : (b + 1) * P],
                     x_tile[:, e * Q : (e + 1) * Q],
                     start=False, stop=(e == E - 1),
                 )
@@ -79,10 +83,8 @@ def tile_rows_placenorm_proj_kernel(tc, a, wd, x, w, s, offs, out):
         inverse_rms = held.tile([P, N], F32)
         nc.scalar.activation(inverse_rms[:], mean[:], ABS_RSQRT, bias=eps[:])
         normed = held.tile([P, MB, N], F32)
-        out_rows = out.rearrange("(p b) n -> p b n", b=MB)
         for b in range(MB):
             nc.vector.scalar_tensor_tensor(
                 normed[:, b, :], windows[b][:], gain[:, b : b + 1], inverse_rms[:], MULT, MULT
             )
-            if b % 2 == 1:
-                nc.sync.dma_start(out_rows[:, b - 1 : b + 1, :], normed[:, b - 1 : b + 1, :])
+            nc.sync.dma_start(out[b * P : (b + 1) * P, :], normed[:, b, :])

@@ -13,8 +13,8 @@ K = 128
 E = 4
 Q = N // E
 EPS = 1e-5
-WARM_COLUMNS = 512
-WARM_MATMULS = 4
+WARM_COLUMNS = 256
+WARM_MATMULS = 8
 DB = D // P
 MB = M // P
 
@@ -31,13 +31,15 @@ def tile_rows_placenorm_proj_kernel(tc, a, wd, x, w, s, offs, out):
         wd_tile = held.tile([P, DB, M], BF16)
         offsets = held.tile([P, N // 16], U16)
         x_tile = held.tile([P, N], BF16)
-        w_tile = held.tile([P, E, M], BF16)
+        w_tiles = [held.tile([P, E, M // 2], BF16, name=f"w{h}") for h in range(2)]
         gain = held.tile([P, MB], F32)
         nc.sync.dma_start(a_tile[:], a.rearrange("(p t) n -> p t n", t=DB))
         nc.sync.dma_start(wd_tile[:], wd.rearrange("(p t) m -> p t m", t=DB))
         nc.sync.dma_start(offsets[:], offs)
         nc.sync.dma_start(x_tile[:], x)
-        nc.sync.dma_start(w_tile[:], w.rearrange("e k m -> k e m"))
+        w_halves = w.rearrange("e k (h m) -> h k e m", h=2)
+        for h in range(2):
+            nc.sync.dma_start(w_tiles[h][:], w_halves[h])
         nc.sync.dma_start(gain[:], s.rearrange("(b p) o -> p (b o)", p=P))
 
         zeros = held.tile([P, WARM_COLUMNS], BF16)
@@ -68,7 +70,7 @@ def tile_rows_placenorm_proj_kernel(tc, a, wd, x, w, s, offs, out):
                 piece = offsets[:, e * (Q // 16) : (e + 1) * (Q // 16)]
                 nc.tensor.matmul(
                     windows[b][:].indirect(piece),
-                    w_tile[:, e, b * P : (b + 1) * P],
+                    w_tiles[b // 2][:, e, (b % 2) * P : (b % 2 + 1) * P],
                     x_tile[:, e * Q : (e + 1) * Q],
                     start=False, stop=(e == E - 1),
                 )

import concourse.mybir as mybir

BF16, F32, U16 = mybir.dt.bfloat16, mybir.dt.float32, mybir.dt.uint16
MULT = mybir.AluOpType.mult
SQUARE = mybir.ActivationFunctionType.Square
ABS_RSQRT = mybir.ActivationFunctionType.Abs_reciprocal_sqrt

P = 128
D = 256
M = 512
N = 256
K = 128
E = 4
Q = N // E
EPS = 1e-5
WARM_COLUMNS = 256
WARM_MATMULS = 8
DB = D // P
MB = M // P

FLOPS = 2 * D * M * N + 2 * K * M * N + 4 * M * N


def tile_rows_placenorm_proj_kernel(tc, a, wd, x, w, s, offs, out):
    nc = tc.nc
    with (
        tc.tile_pool(name="held", bufs=1) as held,
        tc.psum_pool(name="psum", bufs=1) as psum,
    ):
        a_tile = held.tile([P, DB, N], BF16)
        wd_tile = held.tile([P, DB, M], BF16)
        offsets = held.tile([P, N // 16], U16)
        x_tile = held.tile([P, N], BF16)
        w_tiles = [held.tile([P, E, M // 2], BF16, name=f"w{h}") for h in range(2)]
        gain = held.tile([P, MB], F32)
        nc.sync.dma_start(a_tile[:], a.rearrange("(p t) n -> p t n", t=DB))
        nc.sync.dma_start(wd_tile[:], wd.rearrange("(p t) m -> p t m", t=DB))
        nc.sync.dma_start(offsets[:], offs)
        nc.sync.dma_start(x_tile[:], x)
        w_halves = w.rearrange("e k (h m) -> h k e m", h=2)
        for h in range(2):
            nc.sync.dma_start(w_tiles[h][:], w_halves[h])
        nc.sync.dma_start(gain[:], s.rearrange("(b p) o -> p (b o)", p=P))

        zeros = held.tile([P, WARM_COLUMNS], BF16)
        nc.vector.memset(zeros[:], 0.0)

        mean_weights = held.tile([P, P], BF16)
        nc.vector.memset(mean_weights[:], 1.0 / M)
        eps = held.tile([P, 1], F32)
        nc.vector.memset(eps[:], EPS)

        table_load = held.tile([P, 1], F32)
        nc.scalar.activation(table_load[:], eps[:], ABS_RSQRT, bias=eps[:])

        warm_bank = psum.tile([P, WARM_COLUMNS], F32)
        for i in range(WARM_MATMULS):
            nc.tensor.matmul(warm_bank[:], zeros[:, 0:P], zeros[:], start=True, stop=True)

        windows = [psum.tile([P, N], F32, name=f"window{b}") for b in range(MB)]
        for t in range(DB):
            for b in range(MB):
                nc.tensor.matmul(
                    windows[b][:], wd_tile[:, t, b * P : (b + 1) * P], a_tile[:, t, :],
                    start=(t == 0), stop=False,
                )

        for b in range(MB):
            for e in range(E):
                piece = offsets[:, e * (Q // 16) : (e + 1) * (Q // 16)]
                nc.tensor.matmul(
                    windows[b][:].indirect(piece),
                    w_tiles[b // 2][:, e, (b % 2) * P : (b % 2 + 1) * P],
                    x_tile[:, e * Q : (e + 1) * Q],
                    start=False, stop=(e == E - 1),
                )

        squares = held.tile([P, MB, N], BF16)
        for b in range(MB):
            nc.scalar.activation(squares[:, b, :], windows[b][:], SQUARE)
        mean = psum.tile([P, N], F32)
        for b in range(MB):
            nc.tensor.matmul(mean[:], mean_weights[:], squares[:, b, :], start=(b == 0), stop=(b == MB - 1))

        inverse_rms = held.tile([P, N], F32)
        nc.scalar.activation(inverse_rms[:], mean[:], ABS_RSQRT, bias=eps[:])
        normed = held.tile([P, MB, N], F32)
        for b in range(MB):
            nc.vector.scalar_tensor_tensor(
                normed[:, b, :], windows[b][:], gain[:, b : b + 1], inverse_rms[:], MULT, MULT
            )
            nc.sync.dma_start(out[b * P : (b + 1) * P, :], normed[:, b, :])
